import numpy as np
import ml_dtypes


def mxq(x, axis, fmt="e4m3"):
    dtype, down = {"e4m3": (ml_dtypes.float8_e4m3fn, 7), "e5m2": (ml_dtypes.float8_e5m2, 14)}[fmt]
    v = np.moveaxis(np.asarray(x, np.float32).astype(ml_dtypes.bfloat16).astype(np.float64), axis, -1)
    blocks = v.reshape(v.shape[:-1] + (-1, 32))
    amax = np.abs(blocks).max(-1, keepdims=True)
    byte = np.maximum(np.where(amax > 0, np.frexp(amax)[1] - 1 + 127, 0) - down, 1)
    scale = np.exp2(byte - 127.0)
    codes = (blocks / scale).astype(np.float32).astype(dtype).astype(np.float64)
    return np.moveaxis((codes * scale).reshape(v.shape), -1, axis)


WIDE = False


def mx_kscale(k):
    if not WIDE:
        return np.ones(k)
    levels = np.array([24, -24, 12, -12, 0])
    if k % 512:
        return np.exp2(np.random.permutation(np.resize(levels, k // 32))).repeat(32)
    a = np.empty((k // 512, 16))
    for p in range(k // 512):
        a[p, :8] = np.random.permutation(np.resize(levels, 8))
        for g in range(8):
            far = levels[np.abs(levels - a[p, g]) >= 10]
            a[p, g + 8] = far[np.random.randint(len(far))]
    return np.exp2(a.ravel()).repeat(32)


def f64(x):
    return np.asarray(x).astype(np.float64)


def striped(idx):
    return np.tile(idx.reshape(-1, 16).T, (8, 1)).astype(np.uint16)


def unstriped(offs):
    return offs[:16].T.reshape(-1).astype(np.int64)


E2M1 = np.array([0.0, 0.5, 1.0, 1.5, 2.0, 3.0, 4.0, 6.0, -0.0, -0.5, -1.0, -1.5, -2.0, -3.0, -4.0, -6.0])


def pack_weight(w, fmt):
    k, n = w.shape
    w = f64(np.asarray(w, np.float32).astype(ml_dtypes.bfloat16)).reshape(k // 32, 32, n)
    amax = np.abs(w).max(1)
    if fmt == "e4m3":
        byte = np.frexp(amax)[1] - 1 + 127 - 7
    else:
        mant, ex = np.frexp(amax / 6.0)
        byte = np.where(mant > 0.5, ex, ex - 1) + 127
    byte = np.clip(np.where(amax > 0, byte, 1), 1, 254)
    scaled = (w * np.exp2(127.0 - byte)[:, None, :]).reshape(k, n).astype(np.float32)
    by_word = np.ascontiguousarray(scaled.reshape(k // 512, 128, 4, n).transpose(0, 1, 3, 2))
    if fmt == "e4m3":
        words = by_word.astype(ml_dtypes.float8_e4m3fn).view(np.uint8)
    else:
        c = by_word.astype(ml_dtypes.float4_e2m1fn).view(np.uint8) & 0xF
        words = (c[..., 0::2] | (c[..., 1::2] << 4)).reshape(k // 512, 128, 2 * n)
    return np.ascontiguousarray(words), np.ascontiguousarray(byte.astype(np.uint8).reshape(k // 512, 16, n))


def unpack_weight(words, scales, fmt):
    g, _, n = scales.shape
    words = np.ascontiguousarray(words).reshape(g, 128, n, -1)
    if fmt == "e4m3":
        vals = words.view(ml_dtypes.float8_e4m3fn).astype(np.float64)
    else:
        nib = np.empty((g, 128, n, 4), np.uint8)
        nib[..., 0::2] = words & 0xF
        nib[..., 1::2] = words >> 4
        vals = E2M1[nib]
    vals = vals * np.repeat(np.exp2(scales.astype(np.float64) - 127.0), 8, axis=1)[..., None]
    return vals.transpose(0, 1, 3, 2).reshape(g * 512, n)


def pack_table4(v):
    words, scales = pack_weight(v, "e2m1")
    g, t = words.shape[0] // 2, v.shape[1]
    return np.ascontiguousarray(words.reshape(g, 2, 128, t, 2).transpose(0, 2, 3, 1, 4).reshape(g, 128, t, 4)), scales


def unpack_table4(words, scales):
    g, _, t, _ = words.shape
    return unpack_weight(words.reshape(g, 128, t, 2, 2).transpose(0, 3, 1, 2, 4).reshape(2 * g, 128, 2 * t), scales, "e2m1")


def planes(y):
    n, m = y.shape
    v = y.astype(np.float32).astype(ml_dtypes.bfloat16).astype(np.float64).reshape(n // 32, 32, m)
    top = np.abs(v).max(1)
    byte = np.clip(np.where(top > 0, np.frexp(top)[1] - 1 + 127 - 7, 1), 1, 254)
    codes = (v * np.exp2(127.0 - byte)[:, None, :]).reshape(n, m).astype(np.float32).astype(ml_dtypes.float8_e4m3fn).view(np.uint8)
    words = codes.reshape(n // 512, 128, 4, m).transpose(0, 1, 3, 2)
    return np.ascontiguousarray(words), np.ascontiguousarray(byte.astype(np.uint8).reshape(n // 512, 16, m))


def sigm(f):
    return 1.0 / (1.0 + np.exp(-np.maximum(f, -700.0)))


K, N, T, J = 1024, 512, 2048, 1024


def setup_inputs():
    n = np.random.standard_normal
    s = mx_kscale(K)[:, None]
    p_tab = pack_table4(n((K, T)) * s)
    p_wk = pack_weight(n((K, N)) / np.sqrt(K) / s, "e4m3")
    return {
        "tab_words": p_tab[0],
        "tab_scales": p_tab[1],
        "wk_words": p_wk[0],
        "wk_scales": p_wk[1],
        "wv": (n((K, N)) / np.sqrt(K) / s).astype(np.float32),
        "st": (n((N, J))).astype(np.float32),
        "rT": (n((N, T))).astype(np.float32),
        "offs": striped(np.random.permutation(T)[:J]),
    }


def reference(tab_words, tab_scales, wk_words, wk_scales, wv, st, rT, offs):
    idx = unstriped(offs)
    tab_ = unpack_table4(tab_words, tab_scales)[:, idx]
    wk_ = unpack_weight(wk_words, wk_scales, "e4m3")
    wv_ = mxq(f64(wv), 0, "e4m3")
    ke = wk_.T @ tab_
    ve = wv_.T @ tab_
    gate = sigm(ke + f64(st))
    out_0 = f64(rT)[:, idx] + gate * ve
    return (out_0,) + planes(out_0)

@@ -1,0 +1,225 @@
+from contextlib import ExitStack
+
+import concourse.mybir as mybir
+
+K, N, T, J = 1024, 512, 2048, 1024
+FLOPS = 2 * 2 * K * N * J
+
+F32 = mybir.dt.float32
+BF16 = mybir.dt.bfloat16
+I32 = mybir.dt.int32
+U32 = mybir.dt.uint32
+U16 = mybir.dt.uint16
+U8 = mybir.dt.uint8
+FP8X4 = mybir.dt.float8_e4m3fn_x4
+FP4X4 = mybir.dt.float4_e2m1fn_x4
+ACT = mybir.ActivationFunctionType
+ALU = mybir.AluOpType
+
+P = 128
+PACK = 4
+PASSES = K // (P * PACK)
+HALF = 512
+HALVES = J // HALF
+PIECE = 256
+
+
+def tile_list_engram_addLP_kernel(
+    tc, tab_words, tab_scales, wk_words, wk_scales, wv, st, rT, offs, out_0, out_1, out_2
+):
+    nc = tc.nc
+    with ExitStack() as ctx:
+        keep = ctx.enter_context(tc.tile_pool(name="keep", bufs=1))
+        psum = ctx.enter_context(tc.psum_pool(name="psum", bufs=4))
+
+        offsets = keep.tile([P, J // 16], U16, name="offsets")
+        nc.sync.dma_start(offsets[:], offs)
+
+        def picks(first, count):
+            return offsets[:, first // 16 : (first + count) // 16]
+
+        warm = keep.tile([P, 1], F32, name="warm")
+        nc.gpsimd.memset(warm[:], 0.0)
+        warm_out = keep.tile([P, 1], F32, name="warm_out")
+        nc.scalar.activation(out=warm_out[:], in_=warm[:], func=ACT.Sigmoid)
+
+        tab_sc = keep.tile([P, T], U8, name="tab_sc")
+        for q in range(4):
+            nc.sync.dma_start(
+                out=tab_sc[32 * q + 24 : 32 * q + 32, :].bitcast(I32),
+                in_=tab_scales[:, 4 * q : 4 * q + 4, :].bitcast(I32),
+            )
+        wk_sc_raw = keep.tile([P, PASSES * N], U8, name="wk_sc_raw")
+        nc.gpsimd.memset(wk_sc_raw[:].bitcast(I32), 0)
+        for q in range(4):
+            nc.vector.memset(tab_sc[32 * q : 32 * q + 24, :].bitcast(I32), 0)
+        for q in range(4):
+            nc.gpsimd.dma_start(
+                out=wk_sc_raw[32 * q : 32 * q + 4, :].bitcast(I32).rearrange("p (a n) -> p a n", a=PASSES),
+                in_=wk_scales[:, 4 * q : 4 * q + 4, :].bitcast(I32).rearrange("a r n -> r a n"),
+            )
+
+        wk_raw = keep.tile([P, PASSES, N], I32, name="wk_raw")
+        nc.sync.dma_start(out=wk_raw[:], in_=wk_words.rearrange("a p n i -> p a (n i)").bitcast(I32))
+        tab_w = keep.tile([P, T], I32, name="tab_w")
+        nc.sync.dma_start(out=tab_w[:], in_=tab_words[0].rearrange("p t b -> p (t b)").bitcast(I32))
+
+        st_rows = st.rearrange("(p t) j -> p t j", t=PACK)
+        r_rows = rT.rearrange("(p t) c -> p t c", t=PACK)
+        out_rows = out_0.rearrange("(p t) j -> p t j", t=PACK)
+        st_sb = [keep.tile([P, J], F32, name="st%d" % t) for t in range(PACK)]
+        r_sb = [keep.tile([P, T], F32, name="r%d" % t) for t in range(PACK)]
+        wv_rows = wv.rearrange("(a p j) n -> a p j n", a=PASSES, j=PACK)
+        wv_raw = {}
+
+        def load_wv(a, c):
+            raw = keep.tile([P, PACK, N // 2], F32, name="wv_raw%d_%d" % (a, c))
+            nc.sync.dma_start(out=raw[:], in_=wv_rows[a][:, :, c * (N // 2) : (c + 1) * (N // 2)])
+            wv_raw[(a, c)] = raw
+
+        def load_st(t):
+            nc.sync.dma_start(out=st_sb[t][:], in_=st_rows[:, t, :])
+
+        def load_r(t):
+            nc.sync.dma_start(out=r_sb[t][:], in_=r_rows[:, t, :])
+
+        load_wv(0, 0)
+        load_wv(0, 1)
+        load_st(0)
+        load_wv(1, 0)
+        load_wv(1, 1)
+        load_st(1)
+        load_r(0)
+        load_r(1)
+        load_st(2)
+        load_st(3)
+        load_r(2)
+        load_r(3)
+
+        picked_sc = keep.tile([P, J], U8, name="picked_sc")
+        nc.vector.tensor_copy(out=picked_sc[:], in_=tab_sc[:].indirect(offsets[:]))
+        v_sc = []
+        for a in range(PASSES):
+            plane = keep.tile([P, J], U8, name="v_sc%d" % a, align_bytes=64)
+            nc.gpsimd.dma_start(
+                out=plane[0:100, :].bitcast(I32), in_=picked_sc[24 + 4 * a : 124 + 4 * a, :].bitcast(I32)
+            )
+            v_sc.append(plane)
+
+        wk_w = keep.tile([P, PASSES, N], I32, name="wk_w", align_bytes=64)
+        nc.vector.tensor_copy(
+            out=wk_w[:].rearrange("p a (t c i) -> p a c t i", t=PACK, i=4),
+            in_=wk_raw[:].rearrange("p a (c i t) -> p a c t i", t=PACK, i=4),
+        )
+        wk_sc = keep.tile([P, PASSES * N], U8, name="wk_sc", align_bytes=64)
+        nc.vector.tensor_copy(
+            out=wk_sc[:].rearrange("p (a t c i) -> p a c t i", a=PASSES, t=PACK, i=16),
+            in_=wk_sc_raw[:].rearrange("p (a c i t) -> p a c t i", a=PASSES, t=PACK, i=16),
+        )
+
+        v_w = []
+        for h in range(HALVES):
+            pairs = keep.tile([P, HALF], I32, name="pairs%d" % h)
+            nc.vector.tensor_copy(out=pairs[:].bitcast(U32), in_=tab_w[:].bitcast(U32).indirect(picks(h * HALF, HALF)))
+            parted = keep.tile([P, PASSES * 2 * HALF], U8, name="parted%d" % h, align_bytes=64)
+            nc.vector.tensor_copy(
+                out=parted[:].bitcast(U16).rearrange("p (d j) -> p d j", d=PASSES),
+                in_=pairs[:].bitcast(U16).rearrange("p (j d) -> p d j", d=PASSES),
+            )
+            v_w.append(parted)
+
+        wv_w = []
+        wv_sc = []
+        for a in range(PASSES):
+            grouped = keep.tile([P, N * PACK], BF16, name="wv_bf%d" % a, align_bytes=64)
+            for c in range(2):
+                nc.scalar.copy(
+                    out=grouped[:].rearrange("p (t m j) -> p m t j", t=PACK, j=PACK)[:, c * 64 : (c + 1) * 64],
+                    in_=wv_raw[(a, c)][:].rearrange("p j (m t) -> p m t j", t=PACK),
+                )
+            codes = keep.tile([P, N], U32, name="wv_w%d" % a, align_bytes=64)
+            scales = keep.tile([P, N], U8, name="wv_sc%d" % a, align_bytes=64)
+            nc.vector.quantize_mx(out=codes[:].bitcast(FP8X4), scales=scales[:], in_=grouped[:])
+            wv_w.append(codes)
+            wv_sc.append(scales)
+
+        def product(acc, words, scales, h):
+            for a in range(PASSES):
+                nc.tensor.matmul_mx(
+                    out=acc[:],
+                    lhsT=words[a].bitcast(FP8X4),
+                    lhsT_scale=scales[a],
+                    rhs=v_w[h][:, a * 2 * HALF : (a + 1) * 2 * HALF].bitcast(FP4X4),
+                    rhs_scale=v_sc[a][:, h * HALF : (h + 1) * HALF],
+                    start=(a == 0),
+                    stop=(a == PASSES - 1),
+                )
+
+        pieces = [(0, 512), (512, 256), (768, 256)]
+        y_bf = [keep.tile([P, width * PACK], BF16, name="y_bf%d" % j0, align_bytes=64) for j0, width in pieces]
+        y_sc = keep.tile([P, J], U8, name="y_sc", align_bytes=64)
+        out_words = out_1[0].rearrange("p j i -> p (j i)").bitcast(I32)
+
+        def gate_of(t, h):
+            cols = slice(t * P, (t + 1) * P)
+            ke = psum.tile([P, HALF], F32, name="ke")
+            product(
+                ke,
+                [wk_w[:, a, cols] for a in range(PASSES)],
+                [wk_sc[:, a * N + t * P : a * N + (t + 1) * P] for a in range(PASSES)],
+                h,
+            )
+            pre = keep.tile([P, HALF], F32, name="pre%d_%d" % (h, t))
+            nc.vector.tensor_tensor(out=pre[:], in0=ke[:], in1=st_sb[t][:, h * HALF : (h + 1) * HALF], op=ALU.add)
+            gate = keep.tile([P, HALF], F32, name="gate%d_%d" % (h, t))
+            nc.scalar.activation(out=gate[:], in_=pre[:], func=ACT.Sigmoid)
+            return gate
+
+        def gated_value(t, h, gate, m):
+            cols = slice(t * P, (t + 1) * P)
+            ve = psum.tile([P, HALF], F32, name="ve")
+            product(ve, [wv_w[a][:, cols] for a in range(PASSES)], [wv_sc[a][:, cols] for a in range(PASSES)], h)
+            nc.vector.tensor_tensor(out=m[:, h * HALF : (h + 1) * HALF], in0=ve[:], in1=gate[:], op=ALU.mult)
+
+        def add_record(dst, t, m, j0, width):
+            nc.vector.tensor_tensor(
+                out=dst, in0=r_sb[t][:].indirect(picks(j0, width)), in1=m[:, j0 : j0 + width], op=ALU.add
+            )
+
+        def round_pair(u, k, src):
+            nc.scalar.copy(
+                out=y_bf[k][:].rearrange("p (j u e) -> p j u e", u=2, e=2)[:, :, u, :],
+                in_=src.rearrange("p e j -> p j e"),
+            )
+
+        def gated_pair(u):
+            ts = (2 * u, 2 * u + 1)
+            gates = {(t, h): gate_of(t, h) for t in ts for h in range(HALVES)}
+            ms = [keep.tile([P, J], F32, name="gated%d" % t) for t in ts]
+            for e, t in enumerate(ts):
+                for h in range(HALVES):
+                    gated_value(t, h, gates[(t, h)], ms[e])
+            return ms
+
+        ms = gated_pair(0)
+        y_low = keep.tile([P, 2, J], F32, name="y_low")
+        for t in range(2):
+            add_record(y_low[:, t, :], t, ms[t], 0, J)
+            nc.sync.dma_start(out=out_rows[:, t, :], in_=y_low[:, t, :])
+        for k, (j0, width) in enumerate(pieces):
+            round_pair(0, k, y_low[:, :, j0 : j0 + width])
+        ms = gated_pair(1)
+        for k, (j0, width) in enumerate(pieces):
+            y_high = keep.tile([P, 2, width], F32, name="y_high%d" % j0)
+            for e in range(2):
+                add_record(y_high[:, e, :], 2 + e, ms[e], j0, width)
+            nc.sync.dma_start(out=out_rows[:, 2:4, j0 : j0 + width], in_=y_high[:])
+            round_pair(1, k, y_high[:])
+        for k, (j0, width) in enumerate(pieces):
+            y_w = keep.tile([P, width], I32, name="y_w%d" % j0, align_bytes=64)
+            nc.vector.quantize_mx(out=y_w[:].bitcast(FP8X4), scales=y_sc[:, j0 : j0 + width], in_=y_bf[k][:])
+            nc.sync.dma_start(out=out_words[:, j0 : j0 + width], in_=y_w[:])
+        for q in range(4):
+            nc.scalar.dma_start(
+                out=out_2[0, 4 * q : 4 * q + 4, :].bitcast(I32), in_=y_sc[32 * q : 32 * q + 4, :].bitcast(I32)
+            )

@@ -54,72 +54,70 @@ def tile_list_engram_addLP_kernel(
         for q in range(4):
             nc.vector.memset(tab_sc[32 * q : 32 * q + 24, :].bitcast(I32), 0)
         for q in range(4):
-            nc.gpsimd.dma_start(
+            nc.scalar.dma_start(
                 out=wk_sc_raw[32 * q : 32 * q + 4, :].bitcast(I32).rearrange("p (a n) -> p a n", a=PASSES),
                 in_=wk_scales[:, 4 * q : 4 * q + 4, :].bitcast(I32).rearrange("a r n -> r a n"),
             )
 
-        wk_raw = keep.tile([P, PASSES, N], I32, name="wk_raw")
-        nc.sync.dma_start(out=wk_raw[:], in_=wk_words.rearrange("a p n i -> p a (n i)").bitcast(I32))
-        tab_w = keep.tile([P, T], I32, name="tab_w")
+        wk_rows = wk_words.rearrange("a p n i -> a p (n i)").bitcast(I32)
+        wk_raw = []
+        for a in range(PASSES):
+            raw = keep.tile([P, N], I32, name="wk_raw%d" % a, tag="slot_b%d" % a)
+            nc.sync.dma_start(out=raw[:], in_=wk_rows[a])
+            wk_raw.append(raw)
+        tab_w = keep.tile([P, T], I32, name="tab_w", tag="slot_c")
         nc.sync.dma_start(out=tab_w[:], in_=tab_words[0].rearrange("p t b -> p (t b)").bitcast(I32))
 
         st_rows = st.rearrange("(p t) j -> p t j", t=PACK)
         r_rows = rT.rearrange("(p t) c -> p t c", t=PACK)
         out_rows = out_0.rearrange("(p t) j -> p t j", t=PACK)
-        st_sb = [keep.tile([P, J], F32, name="st%d" % t) for t in range(PACK)]
-        r_sb = [keep.tile([P, T], F32, name="r%d" % t) for t in range(PACK)]
         wv_rows = wv.rearrange("(a p j) n -> a p j n", a=PASSES, j=PACK)
         wv_raw = {}
+        st_sb = {}
+        r_sb = {}
 
-        def load_wv(a, c):
-            raw = keep.tile([P, PACK, N // 2], F32, name="wv_raw%d_%d" % (a, c))
+        def load_wv(a, c, tag):
+            raw = keep.tile([P, PACK, N // 2], F32, name="wv_raw%d_%d" % (a, c), tag=tag)
             nc.sync.dma_start(out=raw[:], in_=wv_rows[a][:, :, c * (N // 2) : (c + 1) * (N // 2)])
             wv_raw[(a, c)] = raw
 
-        def load_st(t):
-            nc.sync.dma_start(out=st_sb[t][:], in_=st_rows[:, t, :])
+        def load_st(first, count, tag):
+            rows = keep.tile([P, count, J], F32, name="st%d" % first, tag=tag)
+            nc.sync.dma_start(out=rows[:], in_=st_rows[:, first : first + count, :])
+            for e in range(count):
+                st_sb[first + e] = rows[:, e, :]
 
-        def load_r(t):
+        def load_r(t, tag):
+            r_sb[t] = keep.tile([P, T], F32, name="r%d" % t, tag=tag)
             nc.sync.dma_start(out=r_sb[t][:], in_=r_rows[:, t, :])
 
-        load_wv(0, 0)
-        load_wv(0, 1)
-        load_st(0)
-        load_wv(1, 0)
-        load_wv(1, 1)
-        load_st(1)
-        load_r(0)
-        load_r(1)
-        load_st(2)
-        load_st(3)
-        load_r(2)
-        load_r(3)
+        load_wv(0, 0, "slot_d0")
+        load_wv(0, 1, "slot_d1")
 
         picked_sc = keep.tile([P, J], U8, name="picked_sc")
         nc.vector.tensor_copy(out=picked_sc[:], in_=tab_sc[:].indirect(offsets[:]))
         v_sc = []
         for a in range(PASSES):
             plane = keep.tile([P, J], U8, name="v_sc%d" % a, align_bytes=64)
-            nc.gpsimd.dma_start(
+            (nc.sync if a == 0 else nc.scalar).dma_start(
                 out=plane[0:100, :].bitcast(I32), in_=picked_sc[24 + 4 * a : 124 + 4 * a, :].bitcast(I32)
             )
             v_sc.append(plane)
 
-        wk_w = keep.tile([P, PASSES, N], I32, name="wk_w", align_bytes=64)
-        nc.vector.tensor_copy(
-            out=wk_w[:].rearrange("p a (t c i) -> p a c t i", t=PACK, i=4),
-            in_=wk_raw[:].rearrange("p a (c i t) -> p a c t i", t=PACK, i=4),
-        )
-        wk_sc = keep.tile([P, PASSES * N], U8, name="wk_sc", align_bytes=64)
-        nc.vector.tensor_copy(
-            out=wk_sc[:].rearrange("p (a t c i) -> p a c t i", a=PASSES, t=PACK, i=16),
-            in_=wk_sc_raw[:].rearrange("p (a c i t) -> p a c t i", a=PASSES, t=PACK, i=16),
-        )
 
+        wk_w = keep.tile([P, PASSES, N], I32, name="wk_w", align_bytes=64)
+        for a in range(PASSES):
+            nc.vector.tensor_copy(
+                out=wk_w[:, a, :].rearrange("p (t c i) -> p c t i", t=PACK, i=4),
+                in_=wk_raw[a][:].rearrange("p (c i t) -> p c t i", t=PACK, i=4),
+            )
+            if a == 0:
+                load_st(0, 2, "slot_b0")
+            else:
+                load_wv(1, 0, "slot_b1")
         v_w = []
         for h in range(HALVES):
-            pairs = keep.tile([P, HALF], I32, name="pairs%d" % h)
+            pairs = keep.tile([P, HALF], I32, name="pairs%d" % h, tag="slot_e%d" % h)
             nc.vector.tensor_copy(out=pairs[:].bitcast(U32), in_=tab_w[:].bitcast(U32).indirect(picks(h * HALF, HALF)))
             parted = keep.tile([P, PASSES * 2 * HALF], U8, name="parted%d" % h, align_bytes=64)
             nc.vector.tensor_copy(
@@ -127,9 +125,18 @@ def tile_list_engram_addLP_kernel(
                 in_=pairs[:].bitcast(U16).rearrange("p (j d) -> p d j", d=PASSES),
             )
             v_w.append(parted)
+            if h == 0:
+                load_wv(1, 1, "slot_e0")
+        load_r(0, "slot_c")
 
-        wv_w = []
-        wv_sc = []
+        wk_sc = keep.tile([P, PASSES * N], U8, name="wk_sc", align_bytes=64)
+        nc.vector.tensor_copy(
+            out=wk_sc[:].rearrange("p (a t c i) -> p a c t i", a=PASSES, t=PACK, i=16),
+            in_=wk_sc_raw[:].rearrange("p (a c i t) -> p a c t i", a=PASSES, t=PACK, i=16),
+        )
+
+
+        wv_bf = []
         for a in range(PASSES):
             grouped = keep.tile([P, N * PACK], BF16, name="wv_bf%d" % a, align_bytes=64)
             for c in range(2):
@@ -137,11 +144,20 @@ def tile_list_engram_addLP_kernel(
                     out=grouped[:].rearrange("p (t m j) -> p m t j", t=PACK, j=PACK)[:, c * 64 : (c + 1) * 64],
                     in_=wv_raw[(a, c)][:].rearrange("p j (m t) -> p m t j", t=PACK),
                 )
-            codes = keep.tile([P, N], U32, name="wv_w%d" % a, align_bytes=64)
-            scales = keep.tile([P, N], U8, name="wv_sc%d" % a, align_bytes=64)
-            nc.vector.quantize_mx(out=codes[:].bitcast(FP8X4), scales=scales[:], in_=grouped[:])
-            wv_w.append(codes)
-            wv_sc.append(scales)
+            wv_bf.append(grouped)
+            if a == 0:
+                load_r(1, "slot_d0")
+                load_st(2, 2, "slot_d1")
+            else:
+                load_r(2, "slot_b1")
+                load_r(3, "slot_e0")
+        wv_w = {}
+        wv_sc = {}
+
+        def quantise_wv(a):
+            wv_w[a] = keep.tile([P, N], U32, name="wv_w%d" % a, align_bytes=64)
+            wv_sc[a] = keep.tile([P, N], U8, name="wv_sc%d" % a, align_bytes=64)
+            nc.vector.quantize_mx(out=wv_w[a][:].bitcast(FP8X4), scales=wv_sc[a][:], in_=wv_bf[a][:])
 
         def product(acc, words, scales, h):
             for a in range(PASSES):
@@ -156,7 +172,6 @@ def tile_list_engram_addLP_kernel(
                 )
 
         pieces = [(0, 512), (512, 256), (768, 256)]
-        y_bf = [keep.tile([P, width * PACK], BF16, name="y_bf%d" % j0, align_bytes=64) for j0, width in pieces]
         y_sc = keep.tile([P, J], U8, name="y_sc", align_bytes=64)
         out_words = out_1[0].rearrange("p j i -> p (j i)").bitcast(I32)
 
@@ -169,7 +184,7 @@ def tile_list_engram_addLP_kernel(
                 [wk_sc[:, a * N + t * P : a * N + (t + 1) * P] for a in range(PASSES)],
                 h,
             )
-            pre = keep.tile([P, HALF], F32, name="pre%d_%d" % (h, t))
+            pre = keep.tile([P, HALF], F32, name="pre%d_%d" % (t, h), align_bytes=64)
             nc.vector.tensor_tensor(out=pre[:], in0=ke[:], in1=st_sb[t][:, h * HALF : (h + 1) * HALF], op=ALU.add)
             gate = keep.tile([P, HALF], F32, name="gate%d_%d" % (h, t))
             nc.scalar.activation(out=gate[:], in_=pre[:], func=ACT.Sigmoid)
@@ -181,10 +196,13 @@ def tile_list_engram_addLP_kernel(
             product(ve, [wv_w[a][:, cols] for a in range(PASSES)], [wv_sc[a][:, cols] for a in range(PASSES)], h)
             nc.vector.tensor_tensor(out=m[:, h * HALF : (h + 1) * HALF], in0=ve[:], in1=gate[:], op=ALU.mult)
 
-        def add_record(dst, t, m, j0, width):
-            nc.vector.tensor_tensor(
-                out=dst, in0=r_sb[t][:].indirect(picks(j0, width)), in1=m[:, j0 : j0 + width], op=ALU.add
-            )
+        def pick_record(t, j0, width):
+            rows = keep.tile([P, width], F32, name="picked_r%d_%d" % (t, j0))
+            nc.vector.tensor_copy(out=rows[:], in_=r_sb[t][:].indirect(picks(j0, width)))
+            return rows
+
+        def add_record(dst, rows, m):
+            nc.gpsimd.tensor_tensor(out=dst, in0=rows, in1=m, op=ALU.add)
 
         def round_pair(u, k, src):
             nc.scalar.copy(
@@ -192,29 +210,58 @@ def tile_list_engram_addLP_kernel(
                 in_=src.rearrange("p e j -> p j e"),
             )
 
-        def gated_pair(u):
-            ts = (2 * u, 2 * u + 1)
-            gates = {(t, h): gate_of(t, h) for t in ts for h in range(HALVES)}
-            ms = [keep.tile([P, J], F32, name="gated%d" % t) for t in ts]
-            for e, t in enumerate(ts):
-                for h in range(HALVES):
-                    gated_value(t, h, gates[(t, h)], ms[e])
-            return ms
+        gates = {}
+        ms = [keep.tile([P, J], F32, name="gated%d" % t) for t in range(PACK)]
 
-        ms = gated_pair(0)
+        def gates_of(t):
+            for h in range(HALVES):
+                gates[(t, h)] = gate_of(t, h)
+
+        def values_of(t):
+            for h in range(HALVES):
+                gated_value(t, h, gates[(t, h)], ms[t])
+
         y_low = keep.tile([P, 2, J], F32, name="y_low")
-        for t in range(2):
-            add_record(y_low[:, t, :], t, ms[t], 0, J)
+
+        def finish_low(t, rows):
+            for h in range(HALVES):
+                cols = slice(h * HALF, (h + 1) * HALF)
+                add_record(y_low[:, t, cols], rows[:, cols], ms[t][:, cols])
             nc.sync.dma_start(out=out_rows[:, t, :], in_=y_low[:, t, :])
+
+        quantise_wv(0)
+        gates_of(0)
+        gates_of(1)
+        quantise_wv(1)
+        rows0 = pick_record(0, 0, J)
+        values_of(0)
+        values_of(1)
+        finish_low(0, rows0)
+        rows1 = pick_record(1, 0, J)
+        finish_low(1, rows1)
+        gates_of(2)
+        gates_of(3)
+        rows2 = pick_record(2, 0, J)
+        values_of(2)
+        values_of(3)
+        y_bf = [
+            keep.tile([P, width * PACK], BF16, name="y_bf%d" % j0, tag=tag, align_bytes=64)
+            for (j0, width), tag in zip(pieces, ("pre3_1", "pre3_0", "pre2_1"))
+        ]
         for k, (j0, width) in enumerate(pieces):
             round_pair(0, k, y_low[:, :, j0 : j0 + width])
-        ms = gated_pair(1)
+        y_high = [keep.tile([P, 2, width], F32, name="y_high%d" % j0) for j0, width in pieces]
         for k, (j0, width) in enumerate(pieces):
-            y_high = keep.tile([P, 2, width], F32, name="y_high%d" % j0)
-            for e in range(2):
-                add_record(y_high[:, e, :], 2 + e, ms[e], j0, width)
-            nc.sync.dma_start(out=out_rows[:, 2:4, j0 : j0 + width], in_=y_high[:])
-            round_pair(1, k, y_high[:])
+            add_record(y_high[k][:, 0, :], rows2[:, j0 : j0 + width], ms[2][:, j0 : j0 + width])
+        for k, (j0, width) in enumerate(pieces):
+            nc.vector.tensor_tensor(
+                out=y_high[k][:, 1, :],
+                in0=r_sb[3][:].indirect(picks(j0, width)),
+                in1=ms[3][:, j0 : j0 + width],
+                op=ALU.add,
+            )
+            nc.sync.dma_start(out=out_rows[:, 2:4, j0 : j0 + width], in_=y_high[k][:])
+            round_pair(1, k, y_high[k][:])
         for k, (j0, width) in enumerate(pieces):
             y_w = keep.tile([P, width], I32, name="y_w%d" % j0, align_bytes=64)
             nc.vector.quantize_mx(out=y_w[:].bitcast(FP8X4), scales=y_sc[:, j0 : j0 + width], in_=y_bf[k][:])

@@ -19,9 +19,12 @@ ALU = mybir.AluOpType
 P = 128
 PACK = 4
 PASSES = K // (P * PACK)
+QUADS = 4
 HALF = 512
 HALVES = J // HALF
-PIECE = 256
+PARK = 24
+SPAN = 100
+PIECES = ((0, 512), (512, 256), (768, 256))
 
 
 def tile_list_engram_addLP_kernel(
@@ -29,135 +32,99 @@ def tile_list_engram_addLP_kernel(
 ):
     nc = tc.nc
     with ExitStack() as ctx:
-        keep = ctx.enter_context(tc.tile_pool(name="keep", bufs=1))
+        sb = ctx.enter_context(tc.tile_pool(name="sb", bufs=1))
         psum = ctx.enter_context(tc.psum_pool(name="psum", bufs=4))
 
-        offsets = keep.tile([P, J // 16], U16, name="offsets")
+        st_rows = st.rearrange("(p t) j -> p t j", t=PACK)
+        r_rows = rT.rearrange("(p t) c -> p t c", t=PACK)
+        out_rows = out_0.rearrange("(p t) j -> p t j", t=PACK)
+        wv_rows = wv.rearrange("(a p i) n -> a p i n", a=PASSES, i=PACK)
+        out_words = out_1[0].rearrange("p j i -> p (j i)").bitcast(I32)
+
+        offsets = sb.tile([P, J // 16], U16, name="offsets")
         nc.sync.dma_start(offsets[:], offs)
 
         def picks(first, count):
             return offsets[:, first // 16 : (first + count) // 16]
 
-        warm = keep.tile([P, 1], F32, name="warm")
-        nc.gpsimd.memset(warm[:], 0.0)
-        warm_out = keep.tile([P, 1], F32, name="warm_out")
-        nc.scalar.activation(out=warm_out[:], in_=warm[:], func=ACT.Sigmoid)
-
-        tab_sc = keep.tile([P, T], U8, name="tab_sc")
-        for q in range(4):
+        tab_sc = sb.tile([P, T], U8, name="tab_sc", tag="slot_a")
+        for q in range(QUADS):
             nc.sync.dma_start(
-                out=tab_sc[32 * q + 24 : 32 * q + 32, :].bitcast(I32),
+                out=tab_sc[32 * q + PARK : 32 * q + 32, :].bitcast(I32),
                 in_=tab_scales[:, 4 * q : 4 * q + 4, :].bitcast(I32),
             )
-        wk_sc_raw = keep.tile([P, PASSES * N], U8, name="wk_sc_raw")
+        wk_raw = sb.tile([P, PASSES, N], I32, name="wk_raw", tag="slot_b")
+        nc.sync.dma_start(out=wk_raw[:], in_=wk_words.rearrange("a p n i -> p a (n i)").bitcast(I32))
+        tab_w = sb.tile([P, T], I32, name="tab_w", tag="slot_c")
+        nc.sync.dma_start(out=tab_w[:], in_=tab_words[0].rearrange("p t b -> p (t b)").bitcast(I32))
+
+        def load_st(u, tag):
+            rows = sb.tile([P, 2, J], F32, name="st%d" % u, tag=tag)
+            nc.sync.dma_start(out=rows[:], in_=st_rows[:, 2 * u : 2 * u + 2, :])
+            return rows
+
+        def load_r(t, tag):
+            rows = sb.tile([P, T], F32, name="r%d" % t, tag=tag)
+            nc.sync.dma_start(out=rows[:], in_=r_rows[:, t, :])
+            return rows
+
+        def load_wv(a, first, count, tag):
+            raw = sb.tile([P, PACK, count], F32, name="wv_raw%d_%d" % (a, first), tag=tag)
+            nc.sync.dma_start(out=raw[:], in_=wv_rows[a][:, :, first : first + count])
+            return raw
+
+        st_low = load_st(0, "slot_d")
+
+        warm = sb.tile([P, 1], F32, name="warm")
+        nc.gpsimd.memset(warm[:], 0.0)
+        warm_out = sb.tile([P, 1], F32, name="warm_out")
+        nc.scalar.activation(out=warm_out[:], in_=warm[:], func=ACT.Sigmoid)
+
+        wk_sc_raw = sb.tile([P, PASSES * N], U8, name="wk_sc_raw")
         nc.gpsimd.memset(wk_sc_raw[:].bitcast(I32), 0)
-        for q in range(4):
-            nc.vector.memset(tab_sc[32 * q : 32 * q + 24, :].bitcast(I32), 0)
-        for q in range(4):
+        for q in range(QUADS):
             nc.scalar.dma_start(
                 out=wk_sc_raw[32 * q : 32 * q + 4, :].bitcast(I32).rearrange("p (a n) -> p a n", a=PASSES),
                 in_=wk_scales[:, 4 * q : 4 * q + 4, :].bitcast(I32).rearrange("a r n -> r a n"),
             )
+        for q in range(QUADS):
+            nc.vector.memset(tab_sc[32 * q : 32 * q + PARK, :].bitcast(I32), 0)
 
-        wk_rows = wk_words.rearrange("a p n i -> a p (n i)").bitcast(I32)
-        wk_raw = []
-        for a in range(PASSES):
-            raw = keep.tile([P, N], I32, name="wk_raw%d" % a, tag="slot_b%d" % a)
-            nc.sync.dma_start(out=raw[:], in_=wk_rows[a])
-            wk_raw.append(raw)
-        tab_w = keep.tile([P, T], I32, name="tab_w", tag="slot_c")
-        nc.sync.dma_start(out=tab_w[:], in_=tab_words[0].rearrange("p t b -> p (t b)").bitcast(I32))
-
-        st_rows = st.rearrange("(p t) j -> p t j", t=PACK)
-        r_rows = rT.rearrange("(p t) c -> p t c", t=PACK)
-        out_rows = out_0.rearrange("(p t) j -> p t j", t=PACK)
-        wv_rows = wv.rearrange("(a p j) n -> a p j n", a=PASSES, j=PACK)
-        wv_raw = {}
-        st_sb = {}
-        r_sb = {}
-
-        def load_wv(a, c, tag):
-            raw = keep.tile([P, PACK, N // 2], F32, name="wv_raw%d_%d" % (a, c), tag=tag)
-            nc.sync.dma_start(out=raw[:], in_=wv_rows[a][:, :, c * (N // 2) : (c + 1) * (N // 2)])
-            wv_raw[(a, c)] = raw
-
-        def load_st(first, count, tag):
-            rows = keep.tile([P, count, J], F32, name="st%d" % first, tag=tag)
-            nc.sync.dma_start(out=rows[:], in_=st_rows[:, first : first + count, :])
-            for e in range(count):
-                st_sb[first + e] = rows[:, e, :]
-
-        def load_r(t, tag):
-            r_sb[t] = keep.tile([P, T], F32, name="r%d" % t, tag=tag)
-            nc.sync.dma_start(out=r_sb[t][:], in_=r_rows[:, t, :])
-
-        load_wv(0, 0, "slot_d0")
-        load_wv(0, 1, "slot_d1")
-
-        picked_sc = keep.tile([P, J], U8, name="picked_sc")
+        picked_sc = sb.tile([P, J], U8, name="picked_sc")
         nc.vector.tensor_copy(out=picked_sc[:], in_=tab_sc[:].indirect(offsets[:]))
         v_sc = []
-        for a in range(PASSES):
-            plane = keep.tile([P, J], U8, name="v_sc%d" % a, align_bytes=64)
-            (nc.sync if a == 0 else nc.scalar).dma_start(
-                out=plane[0:100, :].bitcast(I32), in_=picked_sc[24 + 4 * a : 124 + 4 * a, :].bitcast(I32)
-            )
+        for a, queue in enumerate((nc.sync, nc.scalar)):
+            plane = sb.tile([P, J], U8, name="v_sc%d" % a, align_bytes=64)
+            first = PARK + 4 * a
+            queue.dma_start(out=plane[0:SPAN, :].bitcast(I32), in_=picked_sc[first : first + SPAN, :].bitcast(I32))
             v_sc.append(plane)
+        r0 = load_r(0, "slot_a")
 
+        wk_w = sb.tile([P, PASSES, N], I32, name="wk_w", align_bytes=64)
+        nc.vector.tensor_copy(
+            out=wk_w[:].rearrange("p a (t c i) -> p a c t i", t=PACK, i=4),
+            in_=wk_raw[:].rearrange("p a (c i t) -> p a c t i", t=PACK, i=4),
+        )
+        wv_raw0 = load_wv(0, 0, N, "slot_b")
 
-        wk_w = keep.tile([P, PASSES, N], I32, name="wk_w", align_bytes=64)
-        for a in range(PASSES):
-            nc.vector.tensor_copy(
-                out=wk_w[:, a, :].rearrange("p (t c i) -> p c t i", t=PACK, i=4),
-                in_=wk_raw[a][:].rearrange("p (c i t) -> p c t i", t=PACK, i=4),
-            )
-            if a == 0:
-                load_st(0, 2, "slot_b0")
-            else:
-                load_wv(1, 0, "slot_b1")
         v_w = []
         for h in range(HALVES):
-            pairs = keep.tile([P, HALF], I32, name="pairs%d" % h, tag="slot_e%d" % h)
+            pairs = sb.tile([P, HALF], I32, name="pairs%d" % h, tag="slot_e%d" % h)
             nc.vector.tensor_copy(out=pairs[:].bitcast(U32), in_=tab_w[:].bitcast(U32).indirect(picks(h * HALF, HALF)))
-            parted = keep.tile([P, PASSES * 2 * HALF], U8, name="parted%d" % h, align_bytes=64)
+            parted = sb.tile([P, PASSES * 2 * HALF], U8, name="parted%d" % h, align_bytes=64)
             nc.vector.tensor_copy(
                 out=parted[:].bitcast(U16).rearrange("p (d j) -> p d j", d=PASSES),
                 in_=pairs[:].bitcast(U16).rearrange("p (j d) -> p d j", d=PASSES),
             )
             v_w.append(parted)
-            if h == 0:
-                load_wv(1, 1, "slot_e0")
-        load_r(0, "slot_c")
+        r1 = load_r(1, "slot_e0")
+        wv_raw1 = [load_wv(1, 0, N // 2, "slot_c"), load_wv(1, N // 2, N // 2, "slot_e1")]
 
-        wk_sc = keep.tile([P, PASSES * N], U8, name="wk_sc", align_bytes=64)
+        wk_sc = sb.tile([P, PASSES * N], U8, name="wk_sc", align_bytes=64)
         nc.vector.tensor_copy(
             out=wk_sc[:].rearrange("p (a t c i) -> p a c t i", a=PASSES, t=PACK, i=16),
             in_=wk_sc_raw[:].rearrange("p (a c i t) -> p a c t i", a=PASSES, t=PACK, i=16),
         )
-
-
-        wv_bf = []
-        for a in range(PASSES):
-            grouped = keep.tile([P, N * PACK], BF16, name="wv_bf%d" % a, align_bytes=64)
-            for c in range(2):
-                nc.scalar.copy(
-                    out=grouped[:].rearrange("p (t m j) -> p m t j", t=PACK, j=PACK)[:, c * 64 : (c + 1) * 64],
-                    in_=wv_raw[(a, c)][:].rearrange("p j (m t) -> p m t j", t=PACK),
-                )
-            wv_bf.append(grouped)
-            if a == 0:
-                load_r(1, "slot_d0")
-                load_st(2, 2, "slot_d1")
-            else:
-                load_r(2, "slot_b1")
-                load_r(3, "slot_e0")
-        wv_w = {}
-        wv_sc = {}
-
-        def quantise_wv(a):
-            wv_w[a] = keep.tile([P, N], U32, name="wv_w%d" % a, align_bytes=64)
-            wv_sc[a] = keep.tile([P, N], U8, name="wv_sc%d" % a, align_bytes=64)
-            nc.vector.quantize_mx(out=wv_w[a][:].bitcast(FP8X4), scales=wv_sc[a][:], in_=wv_bf[a][:])
 
         def product(acc, words, scales, h):
             for a in range(PASSES):
@@ -171,102 +138,122 @@ def tile_list_engram_addLP_kernel(
                     stop=(a == PASSES - 1),
                 )
 
-        pieces = [(0, 512), (512, 256), (768, 256)]
-        y_sc = keep.tile([P, J], U8, name="y_sc", align_bytes=64)
-        out_words = out_1[0].rearrange("p j i -> p (j i)").bitcast(I32)
-
-        def gate_of(t, h):
-            cols = slice(t * P, (t + 1) * P)
-            ke = psum.tile([P, HALF], F32, name="ke")
-            product(
-                ke,
-                [wk_w[:, a, cols] for a in range(PASSES)],
-                [wk_sc[:, a * N + t * P : a * N + (t + 1) * P] for a in range(PASSES)],
-                h,
-            )
-            pre = keep.tile([P, HALF], F32, name="pre%d_%d" % (t, h), align_bytes=64)
-            nc.vector.tensor_tensor(out=pre[:], in0=ke[:], in1=st_sb[t][:, h * HALF : (h + 1) * HALF], op=ALU.add)
-            gate = keep.tile([P, HALF], F32, name="gate%d_%d" % (h, t))
-            nc.scalar.activation(out=gate[:], in_=pre[:], func=ACT.Sigmoid)
-            return gate
-
-        def gated_value(t, h, gate, m):
-            cols = slice(t * P, (t + 1) * P)
-            ve = psum.tile([P, HALF], F32, name="ve")
-            product(ve, [wv_w[a][:, cols] for a in range(PASSES)], [wv_sc[a][:, cols] for a in range(PASSES)], h)
-            nc.vector.tensor_tensor(out=m[:, h * HALF : (h + 1) * HALF], in0=ve[:], in1=gate[:], op=ALU.mult)
-
-        def pick_record(t, j0, width):
-            rows = keep.tile([P, width], F32, name="picked_r%d_%d" % (t, j0))
-            nc.vector.tensor_copy(out=rows[:], in_=r_sb[t][:].indirect(picks(j0, width)))
-            return rows
-
-        def add_record(dst, rows, m):
-            nc.gpsimd.tensor_tensor(out=dst, in0=rows, in1=m, op=ALU.add)
-
-        def round_pair(u, k, src):
-            nc.scalar.copy(
-                out=y_bf[k][:].rearrange("p (j u e) -> p j u e", u=2, e=2)[:, :, u, :],
-                in_=src.rearrange("p e j -> p j e"),
-            )
-
         gates = {}
-        ms = [keep.tile([P, J], F32, name="gated%d" % t) for t in range(PACK)]
 
-        def gates_of(t):
+        def make_gates(t, st_pair):
             for h in range(HALVES):
-                gates[(t, h)] = gate_of(t, h)
+                ke = psum.tile([P, HALF], F32, name="ke")
+                product(
+                    ke,
+                    [wk_w[:, a, t * P : (t + 1) * P] for a in range(PASSES)],
+                    [wk_sc[:, a * N + t * P : a * N + (t + 1) * P] for a in range(PASSES)],
+                    h,
+                )
+                ring = "pre%d_%d" % (t, h) if t < 2 else "gate%d_%d" % (t - 2, h)
+                pre = sb.tile([P, HALF], F32, name="pre%d_%d" % (t, h), tag=ring, align_bytes=64)
+                nc.vector.tensor_tensor(
+                    out=pre[:], in0=ke[:], in1=st_pair[:, t % 2, h * HALF : (h + 1) * HALF], op=ALU.add
+                )
+                gate = sb.tile([P, HALF], F32, name="gate%d_%d" % (t, h), align_bytes=64)
+                nc.scalar.activation(out=gate[:], in_=pre[:], func=ACT.Sigmoid)
+                gates[(t, h)] = gate
 
-        def values_of(t):
+        wv_bf = {}
+        wv_w = {}
+        wv_sc = {}
+        for a in range(PASSES):
+            for u in range(2):
+                wv_bf[(a, u)] = sb.tile([P, 2 * P * PACK], BF16, name="wv_bf%d_%d" % (a, u), align_bytes=64)
+                wv_w[(a, u)] = sb.tile([P, 2 * P], U32, name="wv_w%d_%d" % (a, u), align_bytes=64)
+                wv_sc[(a, u)] = sb.tile([P, 2 * P], U8, name="wv_sc%d_%d" % (a, u), align_bytes=64)
+
+        def round_wv(a, u, raw, first):
+            count = raw.shape[2] // PACK
+            nc.scalar.copy(
+                out=wv_bf[(a, u)][:].rearrange("p (e m i) -> p m e i", e=2, i=PACK)[:, first : first + count],
+                in_=raw[:].rearrange("p i (m t) -> p m t i", t=PACK)[:, :, 2 * u : 2 * u + 2, :],
+            )
+
+        def quantise_wv(a, u):
+            nc.vector.quantize_mx(out=wv_w[(a, u)][:].bitcast(FP8X4), scales=wv_sc[(a, u)][:], in_=wv_bf[(a, u)][:])
+
+        def gate_values(t, gated):
             for h in range(HALVES):
-                gated_value(t, h, gates[(t, h)], ms[t])
+                ve = psum.tile([P, HALF], F32, name="ve")
+                product(
+                    ve,
+                    [wv_w[(a, t // 2)][:, (t % 2) * P : (t % 2 + 1) * P] for a in range(PASSES)],
+                    [wv_sc[(a, t // 2)][:, (t % 2) * P : (t % 2 + 1) * P] for a in range(PASSES)],
+                    h,
+                )
+                nc.vector.tensor_tensor(
+                    out=gated[:, h * HALF : (h + 1) * HALF], in0=ve[:], in1=gates[(t, h)][:], op=ALU.mult
+                )
 
-        y_low = keep.tile([P, 2, J], F32, name="y_low")
+        def pick_record(t, rows):
+            picked = sb.tile([P, J], F32, name="picked_r%d" % t)
+            nc.vector.tensor_copy(out=picked[:], in_=rows[:].indirect(offsets[:]))
+            return picked
 
-        def finish_low(t, rows):
+        make_gates(0, st_low)
+        make_gates(1, st_low)
+        st_high = load_st(1, "slot_d")
+        picked0 = pick_record(0, r0)
+        r2 = load_r(2, "slot_a")
+        for u in range(2):
+            round_wv(0, u, wv_raw0, 0)
+            quantise_wv(0, u)
+        r3 = load_r(3, "slot_b")
+        picked1 = pick_record(1, r1)
+        for u in range(2):
+            round_wv(1, u, wv_raw1[0], 0)
+        for u in range(2):
+            round_wv(1, u, wv_raw1[1], P // 2)
+            quantise_wv(1, u)
+
+        gated_low = sb.tile([P, 2, J], F32, name="gated_low", tag="slot_e0")
+        y_low = sb.tile([P, 2, J], F32, name="y_low")
+        for t, picked in enumerate((picked0, picked1)):
+            gate_values(t, gated_low[:, t, :])
             for h in range(HALVES):
                 cols = slice(h * HALF, (h + 1) * HALF)
-                add_record(y_low[:, t, cols], rows[:, cols], ms[t][:, cols])
+                nc.gpsimd.tensor_tensor(out=y_low[:, t, cols], in0=picked[:, cols], in1=gated_low[:, t, cols], op=ALU.add)
             nc.sync.dma_start(out=out_rows[:, t, :], in_=y_low[:, t, :])
 
-        quantise_wv(0)
-        gates_of(0)
-        gates_of(1)
-        quantise_wv(1)
-        rows0 = pick_record(0, 0, J)
-        values_of(0)
-        values_of(1)
-        finish_low(0, rows0)
-        rows1 = pick_record(1, 0, J)
-        finish_low(1, rows1)
-        gates_of(2)
-        gates_of(3)
-        rows2 = pick_record(2, 0, J)
-        values_of(2)
-        values_of(3)
-        y_bf = [
-            keep.tile([P, width * PACK], BF16, name="y_bf%d" % j0, tag=tag, align_bytes=64)
-            for (j0, width), tag in zip(pieces, ("pre3_1", "pre3_0", "pre2_1"))
-        ]
-        for k, (j0, width) in enumerate(pieces):
-            round_pair(0, k, y_low[:, :, j0 : j0 + width])
-        y_high = [keep.tile([P, 2, width], F32, name="y_high%d" % j0) for j0, width in pieces]
-        for k, (j0, width) in enumerate(pieces):
-            add_record(y_high[k][:, 0, :], rows2[:, j0 : j0 + width], ms[2][:, j0 : j0 + width])
-        for k, (j0, width) in enumerate(pieces):
-            nc.vector.tensor_tensor(
-                out=y_high[k][:, 1, :],
-                in0=r_sb[3][:].indirect(picks(j0, width)),
-                in1=ms[3][:, j0 : j0 + width],
-                op=ALU.add,
+        make_gates(2, st_high)
+        make_gates(3, st_high)
+        gated_high = sb.tile([P, 2, J], F32, name="gated_high")
+        gate_values(2, gated_high[:, 0, :])
+        gate_values(3, gated_high[:, 1, :])
+
+        def round_pair(u, dst, src):
+            nc.scalar.copy(
+                out=dst[:].rearrange("p (j u e) -> p j u e", u=2, e=2)[:, :, u, :], in_=src.rearrange("p e j -> p j e")
             )
-            nc.sync.dma_start(out=out_rows[:, 2:4, j0 : j0 + width], in_=y_high[k][:])
-            round_pair(1, k, y_high[k][:])
-        for k, (j0, width) in enumerate(pieces):
-            y_w = keep.tile([P, width], I32, name="y_w%d" % j0, align_bytes=64)
-            nc.vector.quantize_mx(out=y_w[:].bitcast(FP8X4), scales=y_sc[:, j0 : j0 + width], in_=y_bf[k][:])
-            nc.sync.dma_start(out=out_words[:, j0 : j0 + width], in_=y_w[:])
-        for q in range(4):
+
+        y_bf = []
+        for k, (j0, width) in enumerate(PIECES):
+            ring = ("gate1_1", "gate1_0", "gate0_1", "gate0_0")[k]
+            rounded = sb.tile([P, width * PACK], BF16, name="y_bf%d" % k, tag=ring, align_bytes=64)
+            round_pair(0, rounded, y_low[:, :, j0 : j0 + width])
+            y_bf.append(rounded)
+
+        y_sc = sb.tile([P, J], U8, name="y_sc", align_bytes=64)
+        for k, (j0, width) in enumerate(PIECES):
+            cols = slice(j0, j0 + width)
+            y_high = sb.tile([P, 2, width], F32, name="y_high%d" % k)
+            for e, rows in enumerate((r2, r3)):
+                nc.vector.tensor_tensor(
+                    out=y_high[:, e, :], in0=rows[:].indirect(picks(j0, width)), in1=gated_high[:, e, cols], op=ALU.add
+                )
+            nc.sync.dma_start(out=out_rows[:, 2:4, cols], in_=y_high[:])
+            round_pair(1, y_bf[k], y_high[:])
+        for k, (j0, width) in enumerate(PIECES):
+            cols = slice(j0, j0 + width)
+            y_w = sb.tile([P, width], I32, name="y_w%d" % k, align_bytes=64)
+            nc.vector.quantize_mx(out=y_w[:].bitcast(FP8X4), scales=y_sc[:, cols], in_=y_bf[k][:])
+            nc.sync.dma_start(out=out_words[:, cols], in_=y_w[:])
+        for q in range(QUADS):
             nc.scalar.dma_start(
                 out=out_2[0, 4 * q : 4 * q + 4, :].bitcast(I32), in_=y_sc[32 * q : 32 * q + 4, :].bitcast(I32)
             )

@@ -68,12 +68,12 @@ def tile_list_engram_addLP_kernel(
             nc.sync.dma_start(out=rows[:], in_=r_rows[:, t, :])
             return rows
 
-        def load_wv(a, first, count, tag):
-            raw = sb.tile([P, PACK, count], F32, name="wv_raw%d_%d" % (a, first), tag=tag)
-            nc.sync.dma_start(out=raw[:], in_=wv_rows[a][:, :, first : first + count])
+        def load_wv(a, tag):
+            raw = sb.tile([P, PACK, N], F32, name="wv_raw%d" % a, tag=tag)
+            nc.sync.dma_start(out=raw[:], in_=wv_rows[a])
             return raw
 
-        st_low = load_st(0, "slot_d")
+        wv_raw = [load_wv(0, "slot_d")]
 
         warm = sb.tile([P, 1], F32, name="warm")
         nc.gpsimd.memset(warm[:], 0.0)
@@ -98,14 +98,14 @@ def tile_list_engram_addLP_kernel(
             first = PARK + 4 * a
             queue.dma_start(out=plane[0:SPAN, :].bitcast(I32), in_=picked_sc[first : first + SPAN, :].bitcast(I32))
             v_sc.append(plane)
-        r0 = load_r(0, "slot_a")
+        wv_raw.append(load_wv(1, "slot_a"))
 
         wk_w = sb.tile([P, PASSES, N], I32, name="wk_w", align_bytes=64)
         nc.vector.tensor_copy(
             out=wk_w[:].rearrange("p a (t c i) -> p a c t i", t=PACK, i=4),
             in_=wk_raw[:].rearrange("p a (c i t) -> p a c t i", t=PACK, i=4),
         )
-        wv_raw0 = load_wv(0, 0, N, "slot_b")
+        st_low = load_st(0, "slot_b")
 
         v_w = []
         for h in range(HALVES):
@@ -117,8 +117,9 @@ def tile_list_engram_addLP_kernel(
                 in_=pairs[:].bitcast(U16).rearrange("p (j d) -> p d j", d=PASSES),
             )
             v_w.append(parted)
-        r1 = load_r(1, "slot_e0")
-        wv_raw1 = [load_wv(1, 0, N // 2, "slot_c"), load_wv(1, N // 2, N // 2, "slot_e1")]
+        r_sb = [load_r(0, "slot_e0")]
+        st_high = load_st(1, "slot_c")
+        r_sb.append(load_r(1, "slot_e1"))
 
         wk_sc = sb.tile([P, PASSES * N], U8, name="wk_sc", align_bytes=64)
         nc.vector.tensor_copy(
@@ -149,12 +150,11 @@ def tile_list_engram_addLP_kernel(
                     [wk_sc[:, a * N + t * P : a * N + (t + 1) * P] for a in range(PASSES)],
                     h,
                 )
-                ring = "pre%d_%d" % (t, h) if t < 2 else "gate%d_%d" % (t - 2, h)
-                pre = sb.tile([P, HALF], F32, name="pre%d_%d" % (t, h), tag=ring, align_bytes=64)
+                pre = sb.tile([P, HALF], F32, name="pre%d_%d" % (t, h), align_bytes=64)
                 nc.vector.tensor_tensor(
                     out=pre[:], in0=ke[:], in1=st_pair[:, t % 2, h * HALF : (h + 1) * HALF], op=ALU.add
                 )
-                gate = sb.tile([P, HALF], F32, name="gate%d_%d" % (t, h), align_bytes=64)
+                gate = sb.tile([P, HALF], F32, name="gate%d_%d" % (t, h))
                 nc.scalar.activation(out=gate[:], in_=pre[:], func=ACT.Sigmoid)
                 gates[(t, h)] = gate
 
@@ -167,11 +167,10 @@ def tile_list_engram_addLP_kernel(
                 wv_w[(a, u)] = sb.tile([P, 2 * P], U32, name="wv_w%d_%d" % (a, u), align_bytes=64)
                 wv_sc[(a, u)] = sb.tile([P, 2 * P], U8, name="wv_sc%d_%d" % (a, u), align_bytes=64)
 
-        def round_wv(a, u, raw, first):
-            count = raw.shape[2] // PACK
-            nc.scalar.copy(
-                out=wv_bf[(a, u)][:].rearrange("p (e m i) -> p m e i", e=2, i=PACK)[:, first : first + count],
-                in_=raw[:].rearrange("p i (m t) -> p m t i", t=PACK)[:, :, 2 * u : 2 * u + 2, :],
+        def round_wv(a, u, copy):
+            copy(
+                out=wv_bf[(a, u)][:].rearrange("p (e m i) -> p m e i", e=2, i=PACK),
+                in_=wv_raw[a][:].rearrange("p i (m t) -> p m t i", t=PACK)[:, :, 2 * u : 2 * u + 2, :],
             )
 
         def quantise_wv(a, u):
@@ -190,38 +189,32 @@ def tile_list_engram_addLP_kernel(
                     out=gated[:, h * HALF : (h + 1) * HALF], in0=ve[:], in1=gates[(t, h)][:], op=ALU.mult
                 )
 
-        def pick_record(t, rows):
-            picked = sb.tile([P, J], F32, name="picked_r%d" % t)
-            nc.vector.tensor_copy(out=picked[:], in_=rows[:].indirect(offsets[:]))
-            return picked
+        def add_record(dst, t, gated, j0, width):
+            nc.vector.tensor_tensor(out=dst, in0=r_sb[t][:].indirect(picks(j0, width)), in1=gated, op=ALU.add)
 
+        round_wv(0, 0, nc.scalar.copy)
+        round_wv(0, 1, nc.scalar.copy)
+        r_sb.append(load_r(2, "slot_d"))
+        quantise_wv(0, 0)
+        quantise_wv(0, 1)
+        round_wv(1, 0, nc.vector.tensor_copy)
+        round_wv(1, 1, nc.scalar.copy)
+        r_sb.append(load_r(3, "slot_a"))
+        quantise_wv(1, 0)
         make_gates(0, st_low)
         make_gates(1, st_low)
-        st_high = load_st(1, "slot_d")
-        picked0 = pick_record(0, r0)
-        r2 = load_r(2, "slot_a")
-        for u in range(2):
-            round_wv(0, u, wv_raw0, 0)
-            quantise_wv(0, u)
-        r3 = load_r(3, "slot_b")
-        picked1 = pick_record(1, r1)
-        for u in range(2):
-            round_wv(1, u, wv_raw1[0], 0)
-        for u in range(2):
-            round_wv(1, u, wv_raw1[1], P // 2)
-            quantise_wv(1, u)
+        quantise_wv(1, 1)
 
-        gated_low = sb.tile([P, 2, J], F32, name="gated_low", tag="slot_e0")
+        gated_low = sb.tile([P, 2, J], F32, name="gated_low")
         y_low = sb.tile([P, 2, J], F32, name="y_low")
-        for t, picked in enumerate((picked0, picked1)):
-            gate_values(t, gated_low[:, t, :])
-            for h in range(HALVES):
-                cols = slice(h * HALF, (h + 1) * HALF)
-                nc.gpsimd.tensor_tensor(out=y_low[:, t, cols], in0=picked[:, cols], in1=gated_low[:, t, cols], op=ALU.add)
-            nc.sync.dma_start(out=out_rows[:, t, :], in_=y_low[:, t, :])
-
+        gate_values(0, gated_low[:, 0, :])
+        gate_values(1, gated_low[:, 1, :])
+        add_record(y_low[:, 0, :], 0, gated_low[:, 0, :], 0, J)
+        nc.sync.dma_start(out=out_rows[:, 0, :], in_=y_low[:, 0, :])
         make_gates(2, st_high)
         make_gates(3, st_high)
+        add_record(y_low[:, 1, :], 1, gated_low[:, 1, :], 0, J)
+        nc.sync.dma_start(out=out_rows[:, 1, :], in_=y_low[:, 1, :])
         gated_high = sb.tile([P, 2, J], F32, name="gated_high")
         gate_values(2, gated_high[:, 0, :])
         gate_values(3, gated_high[:, 1, :])
@@ -233,7 +226,7 @@ def tile_list_engram_addLP_kernel(
 
         y_bf = []
         for k, (j0, width) in enumerate(PIECES):
-            ring = ("gate1_1", "gate1_0", "gate0_1", "gate0_0")[k]
+            ring = ("pre3_1", "pre3_0", "pre2_1")[k]
             rounded = sb.tile([P, width * PACK], BF16, name="y_bf%d" % k, tag=ring, align_bytes=64)
             round_pair(0, rounded, y_low[:, :, j0 : j0 + width])
             y_bf.append(rounded)
@@ -242,10 +235,8 @@ def tile_list_engram_addLP_kernel(
         for k, (j0, width) in enumerate(PIECES):
             cols = slice(j0, j0 + width)
             y_high = sb.tile([P, 2, width], F32, name="y_high%d" % k)
-            for e, rows in enumerate((r2, r3)):
-                nc.vector.tensor_tensor(
-                    out=y_high[:, e, :], in0=rows[:].indirect(picks(j0, width)), in1=gated_high[:, e, cols], op=ALU.add
-                )
+            for e in range(2):
+                add_record(y_high[:, e, :], 2 + e, gated_high[:, e, cols], j0, width)
             nc.sync.dma_start(out=out_rows[:, 2:4, cols], in_=y_high[:])
             round_pair(1, y_bf[k], y_high[:])
         for k, (j0, width) in enumerate(PIECES):

@@ -1,6 +1,7 @@
 from contextlib import ExitStack
 
 import concourse.mybir as mybir
+from concourse.masks import make_identity
 
 K, N, T, J = 1024, 512, 2048, 1024
 FLOPS = 2 * 2 * K * N * J
@@ -87,6 +88,8 @@ def tile_list_engram_addLP_kernel(
                 out=wk_sc_raw[32 * q : 32 * q + 4, :].bitcast(I32).rearrange("p (a n) -> p a n", a=PASSES),
                 in_=wk_scales[:, 4 * q : 4 * q + 4, :].bitcast(I32).rearrange("a r n -> r a n"),
             )
+        identity = sb.tile([P, P], F32, name="identity")
+        make_identity(nc, identity[:])
         for q in range(QUADS):
             nc.vector.memset(tab_sc[32 * q : 32 * q + PARK, :].bitcast(I32), 0)
 
@@ -98,14 +101,14 @@ def tile_list_engram_addLP_kernel(
             first = PARK + 4 * a
             queue.dma_start(out=plane[0:SPAN, :].bitcast(I32), in_=picked_sc[first : first + SPAN, :].bitcast(I32))
             v_sc.append(plane)
-        wv_raw.append(load_wv(1, "slot_a"))
+        st_low = load_st(0, "slot_a")
 
         wk_w = sb.tile([P, PASSES, N], I32, name="wk_w", align_bytes=64)
         nc.vector.tensor_copy(
             out=wk_w[:].rearrange("p a (t c i) -> p a c t i", t=PACK, i=4),
             in_=wk_raw[:].rearrange("p a (c i t) -> p a c t i", t=PACK, i=4),
         )
-        st_low = load_st(0, "slot_b")
+        wv_raw.append(load_wv(1, "slot_b"))
 
         v_w = []
         for h in range(HALVES):
@@ -141,22 +144,54 @@ def tile_list_engram_addLP_kernel(
 
         gates = {}
 
+        def key_product(t, h):
+            ke = psum.tile([P, HALF], F32, name="ke", tag="bank_a")
+            product(
+                ke,
+                [wk_w[:, a, t * P : (t + 1) * P] for a in range(PASSES)],
+                [wk_sc[:, a * N + t * P : a * N + (t + 1) * P] for a in range(PASSES)],
+                h,
+            )
+            return ke
+
         def make_gates(t, st_pair):
             for h in range(HALVES):
-                ke = psum.tile([P, HALF], F32, name="ke")
-                product(
-                    ke,
-                    [wk_w[:, a, t * P : (t + 1) * P] for a in range(PASSES)],
-                    [wk_sc[:, a * N + t * P : a * N + (t + 1) * P] for a in range(PASSES)],
-                    h,
-                )
-                pre = sb.tile([P, HALF], F32, name="pre%d_%d" % (t, h), align_bytes=64)
+                ke = key_product(t, h)
+                pre = sb.tile([P, HALF], F32, name="pre%d_%d" % (t, h))
                 nc.vector.tensor_tensor(
                     out=pre[:], in0=ke[:], in1=st_pair[:, t % 2, h * HALF : (h + 1) * HALF], op=ALU.add
                 )
                 gate = sb.tile([P, HALF], F32, name="gate%d_%d" % (t, h))
                 nc.scalar.activation(out=gate[:], in_=pre[:], func=ACT.Sigmoid)
                 gates[(t, h)] = gate
+
+        def to_sbuf(acc, name):
+            held = sb.tile([P, HALF], F32, name=name)
+            nc.scalar.copy(out=held[:], in_=acc[:])
+            return held
+
+        def turned_gate(t, h, ke_sb, st_pair):
+            pre = psum.tile([P, HALF], F32, name="pre_turned", tag="bank_b")
+            for b in range(HALF // P):
+                cols = slice(b * P, (b + 1) * P)
+                st_cols = slice(h * HALF + b * P, h * HALF + (b + 1) * P)
+                nc.tensor.matmul(
+                    out=pre[:, cols], lhsT=st_pair[:, t % 2, st_cols], rhs=identity[:],
+                    start=True, stop=False, is_transpose=True,
+                )
+                nc.tensor.matmul(
+                    out=pre[:, cols], lhsT=ke_sb[:, cols], rhs=identity[:], start=False, stop=True, is_transpose=True
+                )
+            turned = sb.tile([P, HALF], F32, name="gate_turned%d_%d" % (t, h), align_bytes=64)
+            nc.scalar.activation(out=turned[:], in_=pre[:], func=ACT.Sigmoid)
+            return turned
+
+        def turn_back(turned):
+            gate = psum.tile([P, HALF], F32, name="gate_back", tag="bank_a")
+            for b in range(HALF // P):
+                cols = slice(b * P, (b + 1) * P)
+                nc.tensor.transpose(gate[:, cols], turned[:, cols], identity[:])
+            return gate
 
         wv_bf = {}
         wv_w = {}
@@ -176,18 +211,18 @@ def tile_list_engram_addLP_kernel(
         def quantise_wv(a, u):
             nc.vector.quantize_mx(out=wv_w[(a, u)][:].bitcast(FP8X4), scales=wv_sc[(a, u)][:], in_=wv_bf[(a, u)][:])
 
-        def gate_values(t, gated):
-            for h in range(HALVES):
-                ve = psum.tile([P, HALF], F32, name="ve")
-                product(
-                    ve,
-                    [wv_w[(a, t // 2)][:, (t % 2) * P : (t % 2 + 1) * P] for a in range(PASSES)],
-                    [wv_sc[(a, t // 2)][:, (t % 2) * P : (t % 2 + 1) * P] for a in range(PASSES)],
-                    h,
-                )
-                nc.vector.tensor_tensor(
-                    out=gated[:, h * HALF : (h + 1) * HALF], in0=ve[:], in1=gates[(t, h)][:], op=ALU.mult
-                )
+        def value_product(t, h):
+            ve = psum.tile([P, HALF], F32, name="ve", tag="bank_b")
+            product(
+                ve,
+                [wv_w[(a, t // 2)][:, (t % 2) * P : (t % 2 + 1) * P] for a in range(PASSES)],
+                [wv_sc[(a, t // 2)][:, (t % 2) * P : (t % 2 + 1) * P] for a in range(PASSES)],
+                h,
+            )
+            return ve
+
+        def gate_value(dst, in_psum, in_sbuf):
+            nc.vector.tensor_tensor(out=dst, in0=in_psum[:], in1=in_sbuf[:], op=ALU.mult)
 
         def add_record(dst, t, gated, j0, width):
             nc.vector.tensor_tensor(out=dst, in0=r_sb[t][:].indirect(picks(j0, width)), in1=gated, op=ALU.add)
@@ -197,27 +232,30 @@ def tile_list_engram_addLP_kernel(
         r_sb.append(load_r(2, "slot_d"))
         quantise_wv(0, 0)
         quantise_wv(0, 1)
-        round_wv(1, 0, nc.vector.tensor_copy)
-        round_wv(1, 1, nc.scalar.copy)
-        r_sb.append(load_r(3, "slot_a"))
-        quantise_wv(1, 0)
         make_gates(0, st_low)
         make_gates(1, st_low)
+        round_wv(1, 0, nc.vector.tensor_copy)
+        round_wv(1, 1, nc.scalar.copy)
+        r_sb.append(load_r(3, "slot_b"))
+        quantise_wv(1, 0)
         quantise_wv(1, 1)
 
+        low = [(t, h) for t in (0, 1) for h in range(HALVES)]
+        high = [(t, h) for t in (2, 3) for h in range(HALVES)]
+        ke_sb = {(t, h): to_sbuf(key_product(t, h), "ke_sb%d_%d" % (t, h)) for t, h in high}
         gated_low = sb.tile([P, 2, J], F32, name="gated_low")
+        for t, h in low:
+            gate_value(gated_low[:, t, h * HALF : (h + 1) * HALF], value_product(t, h), gates[(t, h)])
+        ve_sb = {(t, h): to_sbuf(value_product(t, h), "ve_sb%d_%d" % (t, h)) for t, h in high}
+        turned = {(t, h): turned_gate(t, h, ke_sb[(t, h)], st_high) for t, h in high}
+
         y_low = sb.tile([P, 2, J], F32, name="y_low")
-        gate_values(0, gated_low[:, 0, :])
-        gate_values(1, gated_low[:, 1, :])
-        add_record(y_low[:, 0, :], 0, gated_low[:, 0, :], 0, J)
-        nc.sync.dma_start(out=out_rows[:, 0, :], in_=y_low[:, 0, :])
-        make_gates(2, st_high)
-        make_gates(3, st_high)
-        add_record(y_low[:, 1, :], 1, gated_low[:, 1, :], 0, J)
-        nc.sync.dma_start(out=out_rows[:, 1, :], in_=y_low[:, 1, :])
+        for t in range(2):
+            add_record(y_low[:, t, :], t, gated_low[:, t, :], 0, J)
+            nc.sync.dma_start(out=out_rows[:, t, :], in_=y_low[:, t, :])
         gated_high = sb.tile([P, 2, J], F32, name="gated_high")
-        gate_values(2, gated_high[:, 0, :])
-        gate_values(3, gated_high[:, 1, :])
+        for t, h in high:
+            gate_value(gated_high[:, t - 2, h * HALF : (h + 1) * HALF], turn_back(turned[(t, h)]), ve_sb[(t, h)])
 
         def round_pair(u, dst, src):
             nc.scalar.copy(
@@ -226,7 +264,7 @@ def tile_list_engram_addLP_kernel(
 
         y_bf = []
         for k, (j0, width) in enumerate(PIECES):
-            ring = ("pre3_1", "pre3_0", "pre2_1")[k]
+            ring = ("gate_turned3_1", "gate_turned3_0", "gate_turned2_1")[k]
             rounded = sb.tile([P, width * PACK], BF16, name="y_bf%d" % k, tag=ring, align_bytes=64)
             round_pair(0, rounded, y_low[:, :, j0 : j0 + width])
             y_bf.append(rounded)

from contextlib import ExitStack

import concourse.mybir as mybir
from concourse.masks import make_identity

K, N, T, J = 1024, 512, 2048, 1024
FLOPS = 2 * 2 * K * N * J

F32 = mybir.dt.float32
BF16 = mybir.dt.bfloat16
I32 = mybir.dt.int32
U32 = mybir.dt.uint32
U16 = mybir.dt.uint16
U8 = mybir.dt.uint8
FP8X4 = mybir.dt.float8_e4m3fn_x4
FP4X4 = mybir.dt.float4_e2m1fn_x4
ACT = mybir.ActivationFunctionType
ALU = mybir.AluOpType

P = 128
PACK = 4
PASSES = K // (P * PACK)
QUADS = 4
HALF = 512
HALVES = J // HALF
PARK = 24
SPAN = 100
PIECES = ((0, 512), (512, 256), (768, 256))


def tile_list_engram_addLP_kernel(
    tc, tab_words, tab_scales, wk_words, wk_scales, wv, st, rT, offs, out_0, out_1, out_2
):
    nc = tc.nc
    with ExitStack() as ctx:
        sb = ctx.enter_context(tc.tile_pool(name="sb", bufs=1))
        psum = ctx.enter_context(tc.psum_pool(name="psum", bufs=4))

        st_rows = st.rearrange("(p t) j -> p t j", t=PACK)
        r_rows = rT.rearrange("(p t) c -> p t c", t=PACK)
        out_rows = out_0.rearrange("(p t) j -> p t j", t=PACK)
        wv_rows = wv.rearrange("(a p i) n -> a p i n", a=PASSES, i=PACK)
        out_words = out_1[0].rearrange("p j i -> p (j i)").bitcast(I32)

        offsets = sb.tile([P, J // 16], U16, name="offsets")
        nc.sync.dma_start(offsets[:], offs)

        def picks(first, count):
            return offsets[:, first // 16 : (first + count) // 16]

        tab_sc = sb.tile([P, T], U8, name="tab_sc", tag="slot_a")
        for q in range(QUADS):
            nc.sync.dma_start(
                out=tab_sc[32 * q + PARK : 32 * q + 32, :].bitcast(I32),
                in_=tab_scales[:, 4 * q : 4 * q + 4, :].bitcast(I32),
            )
        wk_raw = sb.tile([P, PASSES, N], I32, name="wk_raw", tag="slot_b")
        nc.sync.dma_start(out=wk_raw[:], in_=wk_words.rearrange("a p n i -> p a (n i)").bitcast(I32))
        tab_w = sb.tile([P, T], I32, name="tab_w", tag="slot_c")
        nc.sync.dma_start(out=tab_w[:], in_=tab_words[0].rearrange("p t b -> p (t b)").bitcast(I32))

        def load_st(u, tag):
            rows = sb.tile([P, 2, J], F32, name="st%d" % u, tag=tag)
            nc.sync.dma_start(out=rows[:], in_=st_rows[:, 2 * u : 2 * u + 2, :])
            return rows

        def load_r(t, tag):
            rows = sb.tile([P, T], F32, name="r%d" % t, tag=tag)
            nc.sync.dma_start(out=rows[:], in_=r_rows[:, t, :])
            return rows

        def load_wv(a, tag):
            raw = sb.tile([P, PACK, N], F32, name="wv_raw%d" % a, tag=tag)
            nc.sync.dma_start(out=raw[:], in_=wv_rows[a])
            return raw

        wv_raw = [load_wv(0, "slot_d")]

        warm = sb.tile([P, 1], F32, name="warm")
        nc.gpsimd.memset(warm[:], 0.0)
        warm_out = sb.tile([P, 1], F32, name="warm_out")
        nc.scalar.activation(out=warm_out[:], in_=warm[:], func=ACT.Sigmoid)

        wk_sc_raw = sb.tile([P, PASSES * N], U8, name="wk_sc_raw")
        nc.gpsimd.memset(wk_sc_raw[:].bitcast(I32), 0)
        for q in range(QUADS):
            nc.scalar.dma_start(
                out=wk_sc_raw[32 * q : 32 * q + 4, :].bitcast(I32).rearrange("p (a n) -> p a n", a=PASSES),
                in_=wk_scales[:, 4 * q : 4 * q + 4, :].bitcast(I32).rearrange("a r n -> r a n"),
            )
        identity = sb.tile([P, P], F32, name="identity")
        make_identity(nc, identity[:])
        for q in range(QUADS):
            nc.vector.memset(tab_sc[32 * q : 32 * q + PARK, :].bitcast(I32), 0)

        picked_sc = sb.tile([P, J], U8, name="picked_sc")
        nc.vector.tensor_copy(out=picked_sc[:], in_=tab_sc[:].indirect(offsets[:]))
        v_sc = []
        for a, queue in enumerate((nc.sync, nc.scalar)):
            plane = sb.tile([P, J], U8, name="v_sc%d" % a, align_bytes=64)
            first = PARK + 4 * a
            queue.dma_start(out=plane[0:SPAN, :].bitcast(I32), in_=picked_sc[first : first + SPAN, :].bitcast(I32))
            v_sc.append(plane)
        st_low = load_st(0, "slot_a")

        wk_w = sb.tile([P, PASSES, N], I32, name="wk_w", align_bytes=64)
        nc.vector.tensor_copy(
            out=wk_w[:].rearrange("p a (t c i) -> p a c t i", t=PACK, i=4),
            in_=wk_raw[:].rearrange("p a (c i t) -> p a c t i", t=PACK, i=4),
        )
        wv_raw.append(load_wv(1, "slot_b"))

        v_w = []
        for h in range(HALVES):
            pairs = sb.tile([P, HALF], I32, name="pairs%d" % h, tag="slot_e%d" % h)
            nc.vector.tensor_copy(out=pairs[:].bitcast(U32), in_=tab_w[:].bitcast(U32).indirect(picks(h * HALF, HALF)))
            parted = sb.tile([P, PASSES * 2 * HALF], U8, name="parted%d" % h, align_bytes=64)
            nc.vector.tensor_copy(
                out=parted[:].bitcast(U16).rearrange("p (d j) -> p d j", d=PASSES),
                in_=pairs[:].bitcast(U16).rearrange("p (j d) -> p d j", d=PASSES),
            )
            v_w.append(parted)
        r_sb = [load_r(0, "slot_e0")]
        st_high = load_st(1, "slot_c")
        r_sb.append(load_r(1, "slot_e1"))

        wk_sc = sb.tile([P, PASSES * N], U8, name="wk_sc", align_bytes=64)
        nc.vector.tensor_copy(
            out=wk_sc[:].rearrange("p (a t c i) -> p a c t i", a=PASSES, t=PACK, i=16),
            in_=wk_sc_raw[:].rearrange("p (a c i t) -> p a c t i", a=PASSES, t=PACK, i=16),
        )

        def product(acc, words, scales, h):
            for a in range(PASSES):
                nc.tensor.matmul_mx(
                    out=acc[:],
                    lhsT=words[a].bitcast(FP8X4),
                    lhsT_scale=scales[a],
                    rhs=v_w[h][:, a * 2 * HALF : (a + 1) * 2 * HALF].bitcast(FP4X4),
                    rhs_scale=v_sc[a][:, h * HALF : (h + 1) * HALF],
                    start=(a == 0),
                    stop=(a == PASSES - 1),
                )

        gates = {}

        def key_product(t, h):
            ke = psum.tile([P, HALF], F32, name="ke", tag="bank_a")
            product(
                ke,
                [wk_w[:, a, t * P : (t + 1) * P] for a in range(PASSES)],
                [wk_sc[:, a * N + t * P : a * N + (t + 1) * P] for a in range(PASSES)],
                h,
            )
            return ke

        def make_gates(t, st_pair):
            for h in range(HALVES):
                ke = key_product(t, h)
                pre = sb.tile([P, HALF], F32, name="pre%d_%d" % (t, h))
                nc.vector.tensor_tensor(
                    out=pre[:], in0=ke[:], in1=st_pair[:, t % 2, h * HALF : (h + 1) * HALF], op=ALU.add
                )
                gate = sb.tile([P, HALF], F32, name="gate%d_%d" % (t, h))
                nc.scalar.activation(out=gate[:], in_=pre[:], func=ACT.Sigmoid)
                gates[(t, h)] = gate

        def to_sbuf(acc, name):
            held = sb.tile([P, HALF], F32, name=name)
            nc.scalar.copy(out=held[:], in_=acc[:])
            return held

        def turned_gate(t, h, ke_sb, st_pair):
            pre = psum.tile([P, HALF], F32, name="pre_turned", tag="bank_b")
            for b in range(HALF // P):
                cols = slice(b * P, (b + 1) * P)
                st_cols = slice(h * HALF + b * P, h * HALF + (b + 1) * P)
                nc.tensor.matmul(
                    out=pre[:, cols], lhsT=st_pair[:, t % 2, st_cols], rhs=identity[:],
                    start=True, stop=False, is_transpose=True,
                )
                nc.tensor.matmul(
                    out=pre[:, cols], lhsT=ke_sb[:, cols], rhs=identity[:], start=False, stop=True, is_transpose=True
                )
            turned = sb.tile([P, HALF], F32, name="gate_turned%d_%d" % (t, h), align_bytes=64)
            nc.scalar.activation(out=turned[:], in_=pre[:], func=ACT.Sigmoid)
            return turned

        def turn_back(turned):
            gate = psum.tile([P, HALF], F32, name="gate_back", tag="bank_a")
            for b in range(HALF // P):
                cols = slice(b * P, (b + 1) * P)
                nc.tensor.transpose(gate[:, cols], turned[:, cols], identity[:])
            return gate

        wv_bf = {}
        wv_w = {}
        wv_sc = {}
        for a in range(PASSES):
            for u in range(2):
                wv_bf[(a, u)] = sb.tile([P, 2 * P * PACK], BF16, name="wv_bf%d_%d" % (a, u), align_bytes=64)
                wv_w[(a, u)] = sb.tile([P, 2 * P], U32, name="wv_w%d_%d" % (a, u), align_bytes=64)
                wv_sc[(a, u)] = sb.tile([P, 2 * P], U8, name="wv_sc%d_%d" % (a, u), align_bytes=64)

        def round_wv(a, u, copy):
            copy(
                out=wv_bf[(a, u)][:].rearrange("p (e m i) -> p m e i", e=2, i=PACK),
                in_=wv_raw[a][:].rearrange("p i (m t) -> p m t i", t=PACK)[:, :, 2 * u : 2 * u + 2, :],
            )

        def quantise_wv(a, u):
            nc.vector.quantize_mx(out=wv_w[(a, u)][:].bitcast(FP8X4), scales=wv_sc[(a, u)][:], in_=wv_bf[(a, u)][:])

        def value_product(t, h):
            ve = psum.tile([P, HALF], F32, name="ve", tag="bank_b")
            product(
                ve,
                [wv_w[(a, t // 2)][:, (t % 2) * P : (t % 2 + 1) * P] for a in range(PASSES)],
                [wv_sc[(a, t // 2)][:, (t % 2) * P : (t % 2 + 1) * P] for a in range(PASSES)],
                h,
            )
            return ve

        def gate_value(dst, in_psum, in_sbuf):
            nc.vector.tensor_tensor(out=dst, in0=in_psum[:], in1=in_sbuf[:], op=ALU.mult)

        def add_record(dst, t, gated, j0, width):
            nc.vector.tensor_tensor(out=dst, in0=r_sb[t][:].indirect(picks(j0, width)), in1=gated, op=ALU.add)

        round_wv(0, 0, nc.scalar.copy)
        round_wv(0, 1, nc.scalar.copy)
        r_sb.append(load_r(2, "slot_d"))
        quantise_wv(0, 0)
        quantise_wv(0, 1)
        make_gates(0, st_low)
        make_gates(1, st_low)
        round_wv(1, 0, nc.vector.tensor_copy)
        round_wv(1, 1, nc.scalar.copy)
        r_sb.append(load_r(3, "slot_b"))
        quantise_wv(1, 0)
        quantise_wv(1, 1)

        low = [(t, h) for t in (0, 1) for h in range(HALVES)]
        high = [(t, h) for t in (2, 3) for h in range(HALVES)]
        ke_sb = {(t, h): to_sbuf(key_product(t, h), "ke_sb%d_%d" % (t, h)) for t, h in high}
        gated_low = sb.tile([P, 2, J], F32, name="gated_low")
        for t, h in low:
            gate_value(gated_low[:, t, h * HALF : (h + 1) * HALF], value_product(t, h), gates[(t, h)])
        ve_sb = {(t, h): to_sbuf(value_product(t, h), "ve_sb%d_%d" % (t, h)) for t, h in high}
        turned = {(t, h): turned_gate(t, h, ke_sb[(t, h)], st_high) for t, h in high}

        y_low = sb.tile([P, 2, J], F32, name="y_low")
        for t in range(2):
            add_record(y_low[:, t, :], t, gated_low[:, t, :], 0, J)
            nc.sync.dma_start(out=out_rows[:, t, :], in_=y_low[:, t, :])
        gated_high = sb.tile([P, 2, J], F32, name="gated_high")
        for t, h in high:
            gate_value(gated_high[:, t - 2, h * HALF : (h + 1) * HALF], turn_back(turned[(t, h)]), ve_sb[(t, h)])

        def round_pair(u, dst, src):
            nc.scalar.copy(
                out=dst[:].rearrange("p (j u e) -> p j u e", u=2, e=2)[:, :, u, :], in_=src.rearrange("p e j -> p j e")
            )

        y_bf = []
        for k, (j0, width) in enumerate(PIECES):
            ring = ("gate_turned3_1", "gate_turned3_0", "gate_turned2_1")[k]
            rounded = sb.tile([P, width * PACK], BF16, name="y_bf%d" % k, tag=ring, align_bytes=64)
            round_pair(0, rounded, y_low[:, :, j0 : j0 + width])
            y_bf.append(rounded)

        y_sc = sb.tile([P, J], U8, name="y_sc", align_bytes=64)
        for k, (j0, width) in enumerate(PIECES):
            cols = slice(j0, j0 + width)
            y_high = sb.tile([P, 2, width], F32, name="y_high%d" % k)
            for e in range(2):
                add_record(y_high[:, e, :], 2 + e, gated_high[:, e, cols], j0, width)
            nc.sync.dma_start(out=out_rows[:, 2:4, cols], in_=y_high[:])
            round_pair(1, y_bf[k], y_high[:])
        for k, (j0, width) in enumerate(PIECES):
            cols = slice(j0, j0 + width)
            y_w = sb.tile([P, width], I32, name="y_w%d" % k, align_bytes=64)
            nc.vector.quantize_mx(out=y_w[:].bitcast(FP8X4), scales=y_sc[:, cols], in_=y_bf[k][:])
            nc.sync.dma_start(out=out_words[:, cols], in_=y_w[:])
        for q in range(QUADS):
            nc.scalar.dma_start(
                out=out_2[0, 4 * q : 4 * q + 4, :].bitcast(I32), in_=y_sc[32 * q : 32 * q + 4, :].bitcast(I32)
            )
